import numpy as np, ml_dtypes
CORES = [1,2,5,7,57,58,61,63,73,74,77,79]
N = 12
TK = 128
COEF = [[2,-1,0,0,0,0,1,0,0,0,0,-1],[-1,2,-1,0,0,0,0,1,0,0,0,0],[0,-1,2,-1,0,0,0,0,1,0,0,0],[0,0,-1,2,-1,0,0,0,0,1,0,0],[0,0,0,-1,2,-1,0,0,0,0,1,0],[0,0,0,0,-1,2,-1,0,0,0,0,1],[1,0,0,0,0,-1,2,-1,0,0,0,0],[0,1,0,0,0,0,-1,2,-1,0,0,0],[0,0,1,0,0,0,0,-1,2,-1,0,0],[0,0,0,1,0,0,0,0,-1,2,-1,0],[0,0,0,0,1,0,0,0,0,-1,2,-1],[-1,0,0,0,0,1,0,0,0,0,-1,2]]
def setup_inputs(rng):
    return {"x": rng.standard_normal((N, 128, TK), dtype=np.float32).astype(ml_dtypes.bfloat16), "a": (rng.standard_normal((N, 128, 128), dtype=np.float32) / 11).astype(ml_dtypes.bfloat16)}
def setup_inputs_big(rng):
    d = setup_inputs(rng)
    for k in ("x", "a"): d[k] = (d[k].astype(np.float32) * 1024.0).astype(d[k].dtype)
    return d
def setup_inputs_small(rng):
    d = setup_inputs(rng)
    for k in ("x", "a"): d[k] = (d[k].astype(np.float32) * (1 / 1024.0)).astype(d[k].dtype)
    return d
def setup_inputs_apart(rng):
    d = setup_inputs(rng)
    f = (10.0 ** rng.permutation(np.linspace(-1.5, 1.5, N))).astype(np.float32).reshape(N, 1, 1)
    for k in ("x", "a"): d[k] = (d[k].astype(np.float32) * f).astype(d[k].dtype)
    return d
def reference(x, a):
    X, A = x.astype(np.float64), a.astype(np.float64)
    y = np.stack([A[r].T @ sum(COEF[r][j] * X[j] for j in range(N)) for r in range(N)])
    return {"y": y.astype(ml_dtypes.bfloat16)}

from concourse.bass import DstId, RemoteDMATransfer
from concourse.mybir import AluOpType

N = 12
D = 128
NW = 4

K_HOP = 4
K_OFF = 8
K_ON = 8

SCRATCH = {
    "xs": ("sbuf", [D, D], "bfloat16"),
    "xd": ("dram", [D, D], "bfloat16"),
    "a_sb": ("sbuf", [D, D], "bfloat16"),
    "ys": ("sbuf", [D, D], "bfloat16"),
    "acc": ("psum", [D, D], "float32"),
}
for _i in range(NW):
    SCRATCH["k%d" % _i] = ("sbuf", [D, D], "bfloat16")
    SCRATCH["w%d" % _i] = ("sbuf", [D, D], "bfloat16")
for _i in range(N):
    SCRATCH["land%d" % _i] = ("sbuf", [D, D], "bfloat16")
    SCRATCH["rl%d" % _i] = ("dram", [D, D], "bfloat16")

SEMAPHORES = ["ldd", "ldx", "lda", "fill", "scaled", "mm", "cp", "st", "sent"]
SEMAPHORES += ["arr%d" % _i for _i in range(N)] + ["rar%d" % _i for _i in range(N)]


def _bits(m):
    return [b for b in range(m.bit_length()) if (m >> b) & 1]


def _mask(engs):
    m = 0
    for b in engs:
        m |= 1 << b
    return m


def _pow2(n):
    p = 1
    while p * 2 <= n:
        p *= 2
    return p


def _plan(T, topo):
    cores = list(T.cores)
    n = len(cores)
    coef = T.tables["COEF"]
    need = [[j for j in range(n) if j != r and coef[r][j] != 0] for r in range(n)]
    dests = [[r for r in range(n) if j in need[r]] for j in range(n)]
    direct = [[r for r in dests[j] if topo.may_write(cores[j], cores[r])] for j in range(n)]
    blocked = [(j, r) for j in range(n) for r in dests[j] if not topo.may_write(cores[j], cores[r])]

    port = {}
    busy = {}

    def book(c, d):
        key = (topo.die(c), topo.chip(d))
        port[key] = port.get(key, 0) + 1
        busy[c] = busy.get(c, 0) + 1

    for j in range(n):
        for r in direct[j]:
            if topo.chip(cores[j]) != topo.chip(cores[r]):
                book(cores[j], cores[r])

    def cands(j, r):
        src, dst = cores[j], cores[r]
        able = [c for c in range(topo.CORES_PER_CHIP * topo.CHIPS)
                if topo.chip(c) == topo.chip(src) and c != src and topo.may_write(c, dst)]
        warm = [c for c in able if c in cores]
        near = [c for c in warm if T.rank_of(c) in dests[j]]
        return near or warm or able

    hops = [{} for _ in range(n)]
    for (j, r) in sorted(blocked, key=lambda e: (len(cands(e[0], e[1])), e)):
        dst = cores[r]
        q = min(cands(j, r), key=lambda c: (port.get((topo.die(c), topo.chip(dst)), 0), busy.get(c, 0), c))
        hops[j].setdefault(q, []).append(r)
        book(q, dst)

    def lanes(c):
        narrow = wide = -1
        for d in cores:
            if d != c:
                narrow &= topo.mask(c, d)
                if topo.chip(d) == topo.chip(c):
                    wide &= topo.mask(c, d)
        lo = _bits(narrow)
        return lo, [b for b in _bits(wide) if b not in lo]

    def split(lo, k_all, ranks):
        k = _pow2(min(k_all, len(lo)) // len(ranks))
        return [(lo[i * k:(i + 1) * k], [r]) for i, r in enumerate(ranks)]

    own = []
    fwd = {}
    hop_eng = {}
    arr = {}
    late = {}
    for j in range(n):
        c = cores[j]
        lo, hi = lanes(c)
        off = [r for r in direct[j] if topo.chip(cores[r]) != topo.chip(c)]
        on = [r for r in direct[j] if topo.chip(cores[r]) == topo.chip(c)]
        trs = split(lo, K_OFF, off) if off else []
        if on:
            pool = hi if hi else lo
            trs.append((pool[:_pow2(min(K_ON, len(pool)))], on))
        own.append(trs)
        for engs, ranks in trs:
            for r in ranks:
                arr[(j, r)] = len(engs)
                far = 0 if topo.chip(cores[r]) == topo.chip(c) else (1 if topo.same_plane(topo.chip(c), topo.chip(cores[r])) else 2)
                late[(j, r)] = far + (2 if hops[j] else 0)
        for q in hops[j]:
            both = lo + hi
            hop_eng[(j, q)] = both[:_pow2(min(K_HOP, len(both)))]
            fwd[(j, q)] = split(lanes(q)[0], K_OFF, hops[j][q])
            for engs, ranks in fwd[(j, q)]:
                for r in ranks:
                    arr[(j, r)] = len(engs)
                    late[(j, r)] = 10
    return {"cores": cores, "need": need, "hops": hops, "own": own, "fwd": fwd, "hop_eng": hop_eng,
            "arr": arr, "late": late}


def rank_program(g, core, T, topo):
    P = _plan(T, topo)
    cores = P["cores"]
    rank = T.rank_of(core)
    sem = T.sem
    sent = [0]

    def send(src, name, semname, trs):
        calls = []
        for engs, dcs in trs:
            ids = []
            for d in dcs:
                rid, pid, _se = topo.addr(d)
                ids.append(DstId(rid=rid, pnc=pid))
            calls.append(RemoteDMATransfer(dst_ids=ids, dma_engine_mask=_mask(engs), remote_sem=sem[semname],
                                           srcs=[src], dsts=[T[name][:] for _d in dcs]))
            sent[0] += len(engs)
        g.remote_dma_fused(calls, local_sem=sem.sent)

    if rank is not None:
        hops = P["hops"][rank]
        if hops:
            g.sync.dma_start(T.xd[:], T.x[:]).then_inc(sem.ldd, 16)
        g.sync.dma_start(T.xs[:], T.x[:]).then_inc(sem.ldx, 16)
        g.sync.dma_start(T.a_sb[:], T.a[:]).then_inc(sem.lda, 16)

        if hops:
            g.wait_ge(sem.ldd, 16)
            for q in hops:
                send(T.xd[:], "rl%d" % rank, "rar%d" % rank, [(P["hop_eng"][(rank, q)], [q])])
        g.wait_ge(sem.ldx, 16)
        send(T.xs[:], "land%d" % rank, "arr%d" % rank,
             [(engs, [cores[r] for r in ranks]) for engs, ranks in P["own"][rank]])

    for j in range(len(cores)):
        if core in P["hops"][j]:
            g.wait_ge(sem["rar%d" % j], len(P["hop_eng"][(j, core)]))
            send(T["rl%d" % j][:], "land%d" % j, "arr%d" % j,
                 [(engs, [cores[r] for r in ranks]) for engs, ranks in P["fwd"][(j, core)]])

    if rank is not None:
        row = T.tables["COEF"][rank]
        terms = sorted(P["need"][rank], key=lambda j: (P["late"][(j, rank)], j))
        if row[rank] != 0:
            terms = [rank] + terms
        weights = sorted(set(row[j] for j in terms if row[j] != 1))
        wbuf = {1: T.a_sb}
        v = g.vector
        for i, c in enumerate(weights):
            v.memset(T["k%d" % i][:], float(c)).then_inc(sem.fill, 1)
            wbuf[c] = T["w%d" % i]
        if weights:
            v.wait_ge(sem.fill, len(weights))
        v.wait_ge(sem.lda, 16)
        for i, c in enumerate(weights):
            v.tensor_tensor(T["w%d" % i][:], T.a_sb[:], T["k%d" % i][:], AluOpType.mult).then_inc(sem.scaled, 1)

        t = g.tensor
        t.wait_ge(sem.lda, 16)
        if weights:
            t.wait_ge(sem.scaled, len(weights))
        for i, j in enumerate(terms):
            if j == rank:
                t.wait_ge(sem.ldx, 16)
                rhs = T.xs
            else:
                t.wait_ge(sem["arr%d" % j], P["arr"][(j, rank)])
                rhs = T["land%d" % j]
            mm = t.matmul(T.acc[:], wbuf[row[j]][:], rhs[:], i == 0, i == len(terms) - 1)
        mm.then_inc(sem.mm, 1)

        v.wait_ge(sem.mm, 1)
        v.tensor_copy(T.ys[:], T.acc[:]).then_inc(sem.cp, 1)
        g.sync.wait_ge(sem.cp, 1)
        g.sync.dma_start(T.y[:], T.ys[:]).then_inc(sem.st, 16)
        g.sync.wait_ge(sem.st, 16)

    if sent[0]:
        g.wait_ge(sem.sent, sent[0])
